import numpy as np
import ml_dtypes


def mxq(x, axis, fmt="e4m3"):
    dtype, down = {"e4m3": (ml_dtypes.float8_e4m3fn, 7), "e5m2": (ml_dtypes.float8_e5m2, 14)}[fmt]
    v = np.moveaxis(np.asarray(x, np.float32).astype(ml_dtypes.bfloat16).astype(np.float64), axis, -1)
    blocks = v.reshape(v.shape[:-1] + (-1, 32))
    amax = np.abs(blocks).max(-1, keepdims=True)
    byte = np.maximum(np.where(amax > 0, np.frexp(amax)[1] - 1 + 127, 0) - down, 1)
    scale = np.exp2(byte - 127.0)
    codes = (blocks / scale).astype(np.float32).astype(dtype).astype(np.float64)
    return np.moveaxis((codes * scale).reshape(v.shape), -1, axis)


WIDE = False


def mx_kscale(k):
    if not WIDE:
        return np.ones(k)
    levels = np.array([10, -10, 5, -5, 0])
    if k % 512:
        return np.exp2(np.random.permutation(np.resize(levels, k // 32))).repeat(32)
    a = np.empty((k // 512, 16))
    for p in range(k // 512):
        a[p, :8] = np.random.permutation(np.resize(levels, 8))
        for g in range(8):
            far = levels[np.abs(levels - a[p, g]) >= 10]
            a[p, g + 8] = far[np.random.randint(len(far))]
    return np.exp2(a.ravel()).repeat(32)


def f64(x):
    return np.asarray(x).astype(np.float64)


def striped(idx):
    return np.tile(idx.reshape(-1, 16).T, (8, 1)).astype(np.uint16)


def unstriped(offs):
    return offs[:16].T.reshape(-1).astype(np.int64)


def d_relu(v):
    return (v > 0).astype(np.float64)


K, T, E, C, H, N = 256, 1024, 2, 512, 512, 1024


def by_expert(wq, xq):
    return np.concatenate([wq[e].T @ xq[:, e * C:(e + 1) * C] for e in range(E)], axis=1)


def setup_inputs():
    n = np.random.standard_normal
    slot_token = np.random.permutation(T)[:E * C]
    s = mx_kscale(N)[:, None]
    z = np.ones(T); z[slot_token] = mx_kscale(E * C)
    return {
        "xT": (n((K, T)) * z[None, :]).astype(np.float32),
        "dyT": (n((N, T)) * s).astype(np.float32),
        "a": n((H, E * C)).astype(np.float32),
        "w2": (n((E, N, H)) / np.sqrt(N) / s[None]).astype(np.float32),
        "gate": np.tile(np.random.uniform(0.2, 1.0, E * C) / z[slot_token], (N, 1)).astype(np.float32),
        "offs": striped(slot_token),
    }


def reference(xT, dyT, a, w2, gate, offs):
    idx = unstriped(offs)
    gq = mxq(f64(gate) * f64(dyT)[:, idx], 0, "e4m3")
    dh = by_expert(mxq(f64(w2), 1, "e4m3"), gq)
    da = mxq(dh * d_relu(f64(a)), 1, "e4m3")
    xq = mxq(f64(xT)[:, idx], 1, "e4m3")
    return np.stack([(xq[:, e * C:(e + 1) * C] @ da[:, e * C:(e + 1) * C].T) for e in range(E)])

@@ -1,0 +1,268 @@
+from contextlib import ExitStack
+
+import concourse.mybir as mybir
+from concourse.masks import make_identity
+
+K, T, E, C, H, N = 256, 1024, 2, 512, 512, 1024
+FLOPS = 2 * E * C * H * (N + K)
+BYTES = 4 * (K * T + N * T + H * E * C + E * N * H + E * C + E * K * H) + 2 * 128 * 64
+
+F32 = mybir.dt.float32
+BF16 = mybir.dt.bfloat16
+U32 = mybir.dt.uint32
+U16 = mybir.dt.uint16
+U8 = mybir.dt.uint8
+FP8X4 = mybir.dt.float8_e4m3fn_x4
+ALU = mybir.AluOpType
+
+P = 128
+PACK = 4
+PASS = P * PACK
+PASSES = N // PASS
+HALF = C // 2
+RUN = 4
+RING = 4
+
+
+def tile_moe_mlp_relu_kernel(tc, xT, dyT, a, w2, gate, offs, out):
+    nc = tc.nc
+    with ExitStack() as ctx:
+        keep = ctx.enter_context(tc.tile_pool(name="keep", bufs=1))
+        ring = ctx.enter_context(tc.tile_pool(name="ring", bufs=RING))
+        dh_psum = ctx.enter_context(tc.psum_pool(name="dh_psum", bufs=4))
+        psum = ctx.enter_context(tc.psum_pool(name="psum", bufs=2))
+
+        def held(shape, dtype, name):
+            return keep.tile(shape, dtype, name=name, align_bytes=64)
+
+        offsets = keep.tile([P, E * C // 16], U16, name="offsets")
+        nc.sync.dma_start(offsets[:], offs)
+
+        def slots(first, count):
+            return offsets[:, first // 16 : (first + count) // 16]
+
+        gates, dy, w_raw, a_sb = {}, {}, {}, {}
+
+        def load_gate(e):
+            gates[e] = held([P, C], F32, "gate%d" % e)
+            nc.sync.dma_start(gates[e][:], gate[0:P, e * C : (e + 1) * C])
+
+        def load_dy(g, j):
+            dy[g, j] = held([P, T], F32, "dy%d%d" % (g, j))
+            rows = dyT[g * PASS : (g + 1) * PASS, :].rearrange("(p j) t -> p j t", j=PACK)
+            nc.sync.dma_start(dy[g, j][:], rows[:, j, :])
+
+        def load_w(e, g):
+            w_raw[e, g] = held([P, PACK, H], F32, "w_raw%d%d" % (e, g))
+            nc.sync.dma_start(
+                w_raw[e, g][:], w2[e, g * PASS : (g + 1) * PASS, :].rearrange("(p j) i -> p j i", j=PACK)
+            )
+
+        def load_a(e, pair):
+            a_sb[e, pair] = held([P, 2, C], F32, "a%d%d" % (e, pair))
+            rows = a[pair * 2 * P : (pair + 1) * 2 * P, e * C : (e + 1) * C]
+            nc.sync.dma_start(a_sb[e, pair][:], rows.rearrange("(b m) s -> m b s", m=P))
+
+        x_raw = {}
+        x_pairs = held([P, T, 2], BF16, "x_pairs")
+
+        def load_x(h):
+            x_raw[h] = held([P, 2, T // 2], F32, "x_raw%d" % h)
+            cols = slice(h * T // 2, (h + 1) * T // 2)
+            nc.sync.dma_start(x_raw[h][:], xT[:, cols].rearrange("(p j) t -> p j t", j=2))
+
+        def cast_x(h):
+            interleave(x_pairs[:, h * T // 2 : (h + 1) * T // 2, :], x_raw[h][:])
+
+        load_gate(0)
+        load_dy(0, 0)
+        load_gate(1)
+        load_dy(0, 1)
+        load_dy(0, 2)
+        load_w(0, 0)
+        load_dy(0, 3)
+        load_w(1, 0)
+        load_dy(1, 0)
+        load_w(0, 1)
+        load_dy(1, 1)
+        load_x(0)
+        load_x(1)
+        load_dy(1, 2)
+        load_w(1, 1)
+        load_dy(1, 3)
+        load_a(0, 0)
+        load_a(0, 1)
+        load_a(1, 0)
+        load_a(1, 1)
+
+        identity = held([P, P], F32, "identity")
+        make_identity(nc, identity[:])
+
+        def interleave(dst, src):
+            nc.scalar.copy(
+                out=dst.rearrange("p (c i) j -> p c j i", i=RUN), in_=src.rearrange("p j (c i) -> p c j i", i=RUN)
+            )
+
+        def quantize(grouped, width, name):
+            codes = held([P, width], U32, name + "_codes")
+            scales = held([P, width], U8, name + "_scales")
+            nc.vector.quantize_mx(out=codes[:].bitcast(FP8X4), scales=scales[:], in_=grouped)
+            return codes, scales
+
+        g_bf, g_mx, w_bf, w_mx = {}, {}, {}, {}
+
+        def gather_g(e, g, first, count):
+            gathered = ring.tile([P, PACK, count], F32, name="gathered%d%d%d" % (e, g, first), tag="gathered%d" % count, bufs=(2 if count == C else RING))
+            for j in range(PACK):
+                nc.vector.tensor_tensor(
+                    gathered[:, j, :],
+                    dy[g, j][:].indirect(slots(e * C + first, count)),
+                    gates[e][:, first : first + count],
+                    ALU.mult,
+                )
+            g_bf[e, g, first] = held([P, count, PACK], BF16, "g_bf%d%d%d" % (e, g, first))
+            interleave(g_bf[e, g, first][:], gathered[:])
+
+        def quantize_g(e, g, first, count):
+            codes, scales = quantize(
+                g_bf[e, g, first][:].rearrange("p s j -> p (s j)"), count, "g%d%d%d" % (e, g, first)
+            )
+            for h in range(count // HALF):
+                cols = slice(h * HALF, (h + 1) * HALF)
+                g_mx[e, g, first // HALF + h] = (codes[:, cols], scales[:, cols])
+
+        def cast_w(e, g):
+            w_bf[e, g] = held([P, H, PACK], BF16, "w_bf%d%d" % (e, g))
+            interleave(w_bf[e, g][:], w_raw[e, g][:])
+
+        def quantize_w(e, g):
+            w_mx[e, g] = quantize(w_bf[e, g][:].rearrange("p i j -> p (i j)"), H, "w%d%d" % (e, g))
+
+        da = {}
+
+        def first_product(e, h, pair):
+            if True:
+                if h == 0:
+                    da[e, pair] = held([P, 2, C], BF16, "da%d%d" % (e, pair))
+                dh = dh_psum.tile([P, 2, HALF], F32, name="dh", tag="dh")
+                for b in range(2):
+                    cols = slice((2 * pair + b) * P, (2 * pair + b + 1) * P)
+                    for g in range(PASSES):
+                        nc.tensor.matmul_mx(
+                            out=dh[:, b, :],
+                            lhsT=w_mx[e, g][0][:, cols].bitcast(FP8X4),
+                            lhsT_scale=w_mx[e, g][1][:, cols],
+                            rhs=g_mx[e, g, h][0].bitcast(FP8X4),
+                            rhs_scale=g_mx[e, g, h][1],
+                            start=(g == 0),
+                            stop=(g == PASSES - 1),
+                        )
+                cols = slice(h * HALF, (h + 1) * HALF)
+                nc.vector.scalar_tensor_tensor(
+                    out=da[e, pair][:, :, cols],
+                    in0=a_sb[e, pair][:, :, cols],
+                    scalar=0.0,
+                    in1=dh[:],
+                    op0=ALU.is_gt,
+                    op1=ALU.mult,
+                )
+
+        x_mx, x_bf, da_bf, da_mx = {}, {}, {}, {}
+
+        def make_x(e):
+            words = held([P, C], U32, "x_words%d" % e)
+            window = x_pairs[:].rearrange("p t j -> p (t j)").bitcast(U32)
+            nc.vector.tensor_copy(words[:], window.indirect(slots(e * C, C)))
+            turned = psum.tile([P, PACK, P], F32, name="x_turned", tag="turned")
+            for t in range(PACK):
+                nc.tensor.transpose(turned[:, t, :], words[:].bitcast(F32)[:, t::PACK], identity[:])
+            grouped = held([P, K, PACK], BF16, "x_bf%d" % e)
+            values = turned[:].rearrange("p t w -> p (t w)").bitcast(BF16)
+            nc.scalar.copy(out=grouped[:], in_=values.rearrange("p (t k) -> p k t", t=PACK))
+            x_bf[e] = grouped
+
+        def quantize_x(e):
+            x_mx[e] = quantize(x_bf[e][:].rearrange("p k t -> p (k t)"), K, "x%d" % e)
+
+        def turn_da(e, pair):
+            turned = psum.tile([P, 2, 2, P], F32, name="da_turned", tag="turned")
+            for b in range(2):
+                words = da[e, pair][:, b, :].bitcast(F32)
+                for u in range(2):
+                    nc.tensor.transpose(turned[:, b, u, :], words[:, u::2], identity[:])
+            grouped = held([P, 2 * P * PACK], BF16, "da_bf%d%d" % (e, pair))
+            nc.scalar.copy(
+                out=grouped[:].bitcast(F32).rearrange("p (b m u) -> p b m u", b=2, u=2),
+                in_=turned[:].rearrange("p b u m -> p b m u"),
+            )
+            da_bf[e, pair] = grouped
+
+        def quantize_da(e, pair):
+            da_mx[e, pair] = quantize(da_bf[e, pair][:], 2 * P, "da%d%d" % (e, pair))
+
+        def second_product(e, pair):
+            codes, scales = da_mx[e, pair]
+            acc = psum.tile([P, K // P, 2 * P], F32, name="acc", tag="acc")
+            for kb in range(K // P):
+                cols = slice(kb * P, (kb + 1) * P)
+                nc.tensor.matmul_mx(
+                    out=acc[:, kb, :],
+                    lhsT=x_mx[e][0][:, cols].bitcast(FP8X4),
+                    lhsT_scale=x_mx[e][1][:, cols],
+                    rhs=codes[:].bitcast(FP8X4),
+                    rhs_scale=scales[:],
+                    start=True,
+                    stop=True,
+                )
+            result = held([P, K // P, 2 * P], F32, "result%d%d" % (e, pair))
+            nc.scalar.copy(out=result[:], in_=acc[:])
+            nc.sync.dma_start(
+                out[e, :, pair * 2 * P : (pair + 1) * 2 * P].rearrange("(kb m) i -> m kb i", m=P), result[:]
+            )
+
+        cast_w(0, 0)
+        cast_w(1, 0)
+        cast_w(0, 1)
+        cast_w(1, 1)
+        quantize_w(0, 0)
+        quantize_w(1, 0)
+        quantize_w(0, 1)
+        quantize_w(1, 1)
+        gather_g(0, 0, 0, C)
+        gather_g(1, 0, 0, C)
+        quantize_g(0, 0, 0, C)
+        quantize_g(1, 0, 0, C)
+        gather_g(0, 1, 0, HALF)
+        gather_g(0, 1, HALF, HALF)
+        gather_g(1, 1, 0, HALF)
+        gather_g(1, 1, HALF, HALF)
+        quantize_g(0, 1, 0, HALF)
+        quantize_g(0, 1, HALF, HALF)
+        cast_x(0)
+        cast_x(1)
+        make_x(0)
+        make_x(1)
+        first_product(0, 0, 0)
+        first_product(0, 0, 1)
+        quantize_g(1, 1, 0, HALF)
+        first_product(0, 1, 0)
+        first_product(0, 1, 1)
+        quantize_g(1, 1, HALF, HALF)
+        first_product(1, 0, 0)
+        first_product(1, 0, 1)
+        quantize_x(0)
+        quantize_x(1)
+        turn_da(0, 0)
+        turn_da(0, 1)
+        first_product(1, 1, 0)
+        first_product(1, 1, 1)
+        quantize_da(0, 0)
+        quantize_da(0, 1)
+        turn_da(1, 0)
+        turn_da(1, 1)
+        second_product(0, 0)
+        second_product(0, 1)
+        quantize_da(1, 0)
+        quantize_da(1, 1)
+        second_product(1, 0)
+        second_product(1, 1)

@@ -5,7 +5,7 @@ from concourse.masks import make_identity
 
 K, T, E, C, H, N = 256, 1024, 2, 512, 512, 1024
 FLOPS = 2 * E * C * H * (N + K)
-BYTES = 4 * (K * T + N * T + H * E * C + E * N * H + E * C + E * K * H) + 2 * 128 * 64
+BYTES = 4 * (K * T + N * T + H * E * C + E * N * H + E * C + E * K * H) + 2 * 128 * (E * C // 16)
 
 F32 = mybir.dt.float32
 BF16 = mybir.dt.bfloat16
@@ -14,255 +14,229 @@ U16 = mybir.dt.uint16
 U8 = mybir.dt.uint8
 FP8X4 = mybir.dt.float8_e4m3fn_x4
 ALU = mybir.AluOpType
+COPY = mybir.ActivationFunctionType.Copy
 
 P = 128
 PACK = 4
 PASS = P * PACK
 PASSES = N // PASS
-HALF = C // 2
-RUN = 4
-RING = 4
+LIST_ROWS = 16
+I_BLOCKS = H // P
+K_BLOCKS = K // P
+PAIR = 2
+RUN = 2
 
 
 def tile_moe_mlp_relu_kernel(tc, xT, dyT, a, w2, gate, offs, out):
     nc = tc.nc
+    experts = range(E)
+    pairs = [(e, first) for e in experts for first in range(0, I_BLOCKS, PAIR)]
+    last_pass = PASSES - 1
+
     with ExitStack() as ctx:
-        keep = ctx.enter_context(tc.tile_pool(name="keep", bufs=1))
-        ring = ctx.enter_context(tc.tile_pool(name="ring", bufs=RING))
-        dh_psum = ctx.enter_context(tc.psum_pool(name="dh_psum", bufs=4))
-        psum = ctx.enter_context(tc.psum_pool(name="psum", bufs=2))
+        sbuf = ctx.enter_context(tc.tile_pool(name="sbuf", bufs=1))
+        psum = ctx.enter_context(tc.psum_pool(name="psum", bufs=1))
 
         def held(shape, dtype, name):
-            return keep.tile(shape, dtype, name=name, align_bytes=64)
+            return sbuf.tile(shape, dtype, name=name, align_bytes=64)
 
-        offsets = keep.tile([P, E * C // 16], U16, name="offsets")
-        nc.sync.dma_start(offsets[:], offs)
+        def bank(shape, number, name):
+            return psum.tile(shape, F32, name=name, tag="bank%d" % number)
 
-        def slots(first, count):
-            return offsets[:, first // 16 : (first + count) // 16]
+        def dh_bank(e, b):
+            return I_BLOCKS * e + b
 
-        gates, dy, w_raw, a_sb = {}, {}, {}, {}
+        offsets = sbuf.tile([P, E * C // LIST_ROWS], U16, name="offsets")
+
+        def slots(e, first, count):
+            start = e * C + first
+            return offsets[:, start // LIST_ROWS : (start + count) // LIST_ROWS]
+
+        gates, dy, x_raw, w_raw, a_sb = {}, {}, {}, {}, {}
 
         def load_gate(e):
             gates[e] = held([P, C], F32, "gate%d" % e)
             nc.sync.dma_start(gates[e][:], gate[0:P, e * C : (e + 1) * C])
 
-        def load_dy(g, j):
-            dy[g, j] = held([P, T], F32, "dy%d%d" % (g, j))
-            rows = dyT[g * PASS : (g + 1) * PASS, :].rearrange("(p j) t -> p j t", j=PACK)
-            nc.sync.dma_start(dy[g, j][:], rows[:, j, :])
+        def load_dy(g, t):
+            dy[g, t] = held([P, T], F32, "dy%d%d" % (g, t))
+            rows = dyT[g * PASS : (g + 1) * PASS, :].rearrange("(p t) c -> p t c", t=PACK)
+            nc.sync.dma_start(dy[g, t][:], rows[:, t, :])
+
+        def load_x(kb):
+            x_raw[kb] = held([P, T], F32, "x_raw%d" % kb)
+            nc.sync.dma_start(x_raw[kb][:], xT[kb * P : (kb + 1) * P, :])
 
         def load_w(e, g):
             w_raw[e, g] = held([P, PACK, H], F32, "w_raw%d%d" % (e, g))
-            nc.sync.dma_start(
-                w_raw[e, g][:], w2[e, g * PASS : (g + 1) * PASS, :].rearrange("(p j) i -> p j i", j=PACK)
-            )
+            rows = w2[e, g * PASS : (g + 1) * PASS, :]
+            nc.sync.dma_start(w_raw[e, g][:], rows.rearrange("(p t) i -> p t i", t=PACK))
 
-        def load_a(e, pair):
-            a_sb[e, pair] = held([P, 2, C], F32, "a%d%d" % (e, pair))
-            rows = a[pair * 2 * P : (pair + 1) * 2 * P, e * C : (e + 1) * C]
-            nc.sync.dma_start(a_sb[e, pair][:], rows.rearrange("(b m) s -> m b s", m=P))
+        def load_a(e, first):
+            a_sb[e, first] = held([P, PAIR, C], F32, "a%d%d" % (e, first))
+            rows = a[first * P : (first + PAIR) * P, e * C : (e + 1) * C]
+            nc.sync.dma_start(a_sb[e, first][:], rows.rearrange("(b m) s -> m b s", m=P))
 
-        x_raw = {}
-        x_pairs = held([P, T, 2], BF16, "x_pairs")
-
-        def load_x(h):
-            x_raw[h] = held([P, 2, T // 2], F32, "x_raw%d" % h)
-            cols = slice(h * T // 2, (h + 1) * T // 2)
-            nc.sync.dma_start(x_raw[h][:], xT[:, cols].rearrange("(p j) t -> p j t", j=2))
-
-        def cast_x(h):
-            interleave(x_pairs[:, h * T // 2 : (h + 1) * T // 2, :], x_raw[h][:])
-
-        load_gate(0)
         load_dy(0, 0)
+        load_gate(0)
+        nc.sync.dma_start(offsets[:], offs)
+        load_x(0)
         load_gate(1)
+        load_x(1)
         load_dy(0, 1)
         load_dy(0, 2)
-        load_w(0, 0)
-        load_dy(0, 3)
-        load_w(1, 0)
         load_dy(1, 0)
-        load_w(0, 1)
+        for e in experts:
+            load_w(e, 0)
+        load_dy(0, 3)
         load_dy(1, 1)
-        load_x(0)
-        load_x(1)
         load_dy(1, 2)
-        load_w(1, 1)
+        for e in experts:
+            load_w(e, 1)
         load_dy(1, 3)
-        load_a(0, 0)
-        load_a(0, 1)
-        load_a(1, 0)
-        load_a(1, 1)
+        for e, first in pairs:
+            load_a(e, first)
 
         identity = held([P, P], F32, "identity")
         make_identity(nc, identity[:])
 
-        def interleave(dst, src):
+        def interleave(grouped, planes):
             nc.scalar.copy(
-                out=dst.rearrange("p (c i) j -> p c j i", i=RUN), in_=src.rearrange("p j (c i) -> p c j i", i=RUN)
+                out=grouped.rearrange("p (c r) t -> p c t r", r=RUN),
+                in_=planes.rearrange("p t (c r) -> p c t r", r=RUN),
             )
 
-        def quantize(grouped, width, name):
-            codes = held([P, width], U32, name + "_codes")
-            scales = held([P, width], U8, name + "_scales")
-            nc.vector.quantize_mx(out=codes[:].bitcast(FP8X4), scales=scales[:], in_=grouped)
-            return codes, scales
+        def mx_tiles(width, name):
+            return held([P, width], U32, name + "_codes"), held([P, width], U8, name + "_scales")
 
-        g_bf, g_mx, w_bf, w_mx = {}, {}, {}, {}
+        def quantize(codes, scales, grouped):
+            nc.vector.quantize_mx(out=codes.bitcast(FP8X4), scales=scales, in_=grouped)
 
-        def gather_g(e, g, first, count):
-            gathered = ring.tile([P, PACK, count], F32, name="gathered%d%d%d" % (e, g, first), tag="gathered%d" % count, bufs=(2 if count == C else RING))
-            for j in range(PACK):
-                nc.vector.tensor_tensor(
-                    gathered[:, j, :],
-                    dy[g, j][:].indirect(slots(e * C + first, count)),
-                    gates[e][:, first : first + count],
-                    ALU.mult,
-                )
-            g_bf[e, g, first] = held([P, count, PACK], BF16, "g_bf%d%d%d" % (e, g, first))
-            interleave(g_bf[e, g, first][:], gathered[:])
-
-        def quantize_g(e, g, first, count):
-            codes, scales = quantize(
-                g_bf[e, g, first][:].rearrange("p s j -> p (s j)"), count, "g%d%d%d" % (e, g, first)
+        def multiply(acc, stationary, cols, moving, start, stop):
+            nc.tensor.matmul_mx(
+                out=acc,
+                lhsT=stationary[0][:, cols].bitcast(FP8X4),
+                lhsT_scale=stationary[1][:, cols],
+                rhs=moving[0][:].bitcast(FP8X4),
+                rhs_scale=moving[1][:],
+                start=start,
+                stop=stop,
             )
-            for h in range(count // HALF):
-                cols = slice(h * HALF, (h + 1) * HALF)
-                g_mx[e, g, first // HALF + h] = (codes[:, cols], scales[:, cols])
 
-        def cast_w(e, g):
-            w_bf[e, g] = held([P, H, PACK], BF16, "w_bf%d%d" % (e, g))
-            interleave(w_bf[e, g][:], w_raw[e, g][:])
-
-        def quantize_w(e, g):
-            w_mx[e, g] = quantize(w_bf[e, g][:].rearrange("p i j -> p (i j)"), H, "w%d%d" % (e, g))
-
-        da = {}
-
-        def first_product(e, h, pair):
-            if True:
-                if h == 0:
-                    da[e, pair] = held([P, 2, C], BF16, "da%d%d" % (e, pair))
-                dh = dh_psum.tile([P, 2, HALF], F32, name="dh", tag="dh")
-                for b in range(2):
-                    cols = slice((2 * pair + b) * P, (2 * pair + b + 1) * P)
-                    for g in range(PASSES):
-                        nc.tensor.matmul_mx(
-                            out=dh[:, b, :],
-                            lhsT=w_mx[e, g][0][:, cols].bitcast(FP8X4),
-                            lhsT_scale=w_mx[e, g][1][:, cols],
-                            rhs=g_mx[e, g, h][0].bitcast(FP8X4),
-                            rhs_scale=g_mx[e, g, h][1],
-                            start=(g == 0),
-                            stop=(g == PASSES - 1),
-                        )
-                cols = slice(h * HALF, (h + 1) * HALF)
-                nc.vector.scalar_tensor_tensor(
-                    out=da[e, pair][:, :, cols],
-                    in0=a_sb[e, pair][:, :, cols],
-                    scalar=0.0,
-                    in1=dh[:],
-                    op0=ALU.is_gt,
-                    op1=ALU.mult,
-                )
-
-        x_mx, x_bf, da_bf, da_mx = {}, {}, {}, {}
-
-        def make_x(e):
-            words = held([P, C], U32, "x_words%d" % e)
-            window = x_pairs[:].rearrange("p t j -> p (t j)").bitcast(U32)
-            nc.vector.tensor_copy(words[:], window.indirect(slots(e * C, C)))
-            turned = psum.tile([P, PACK, P], F32, name="x_turned", tag="turned")
-            for t in range(PACK):
-                nc.tensor.transpose(turned[:, t, :], words[:].bitcast(F32)[:, t::PACK], identity[:])
-            grouped = held([P, K, PACK], BF16, "x_bf%d" % e)
-            values = turned[:].rearrange("p t w -> p (t w)").bitcast(BF16)
-            nc.scalar.copy(out=grouped[:], in_=values.rearrange("p (t k) -> p k t", t=PACK))
-            x_bf[e] = grouped
-
-        def quantize_x(e):
-            x_mx[e] = quantize(x_bf[e][:].rearrange("p k t -> p (k t)"), K, "x%d" % e)
-
-        def turn_da(e, pair):
-            turned = psum.tile([P, 2, 2, P], F32, name="da_turned", tag="turned")
-            for b in range(2):
-                words = da[e, pair][:, b, :].bitcast(F32)
+        def turn(row_blocks, bank_number, name):
+            turned = bank([P, 2, 2, P], bank_number, name + "_turned")
+            for b, rows in enumerate(row_blocks):
+                words = rows[:].bitcast(F32)
                 for u in range(2):
                     nc.tensor.transpose(turned[:, b, u, :], words[:, u::2], identity[:])
-            grouped = held([P, 2 * P * PACK], BF16, "da_bf%d%d" % (e, pair))
+            grouped = held([P, 2 * P * PACK], BF16, name + "_grouped")
             nc.scalar.copy(
                 out=grouped[:].bitcast(F32).rearrange("p (b m u) -> p b m u", b=2, u=2),
                 in_=turned[:].rearrange("p b u m -> p b m u"),
             )
-            da_bf[e, pair] = grouped
+            return grouped
 
-        def quantize_da(e, pair):
-            da_mx[e, pair] = quantize(da_bf[e, pair][:], 2 * P, "da%d%d" % (e, pair))
+        g_grouped, g_mx, dh = {}, {}, {}
 
-        def second_product(e, pair):
-            codes, scales = da_mx[e, pair]
-            acc = psum.tile([P, K // P, 2 * P], F32, name="acc", tag="acc")
-            for kb in range(K // P):
-                cols = slice(kb * P, (kb + 1) * P)
-                nc.tensor.matmul_mx(
-                    out=acc[:, kb, :],
-                    lhsT=x_mx[e][0][:, cols].bitcast(FP8X4),
-                    lhsT_scale=x_mx[e][1][:, cols],
-                    rhs=codes[:].bitcast(FP8X4),
-                    rhs_scale=scales[:],
-                    start=True,
-                    stop=True,
+        def gather_g(e, g, parts):
+            width = C // parts
+            gathered = held([P, PACK, C], F32, "gathered%d%d" % (e, g))
+            for t in range(PACK):
+                count = width if t == PACK - 1 else C
+                for first in range(0, C, count):
+                    nc.vector.tensor_tensor(
+                        gathered[:, t, first : first + count],
+                        dy[g, t][:].indirect(slots(e, first, count)),
+                        gates[e][:, first : first + count],
+                        ALU.mult,
+                    )
+            g_grouped[e, g] = []
+            for first in range(0, C, width):
+                grouped = held([P, width, PACK], BF16, "g_grouped%d%d_%d" % (e, g, first))
+                interleave(grouped[:], gathered[:, :, first : first + width])
+                g_grouped[e, g].append((slice(first, first + width), grouped))
+
+        def quantize_g(e, g):
+            g_mx[e, g] = mx_tiles(C, "g%d%d" % (e, g))
+            codes, scales = g_mx[e, g]
+            for cols, grouped in g_grouped[e, g]:
+                quantize(codes[:, cols], scales[:, cols], grouped[:].rearrange("p s t -> p (s t)"))
+
+        def first_product(e, g):
+            for b in range(I_BLOCKS):
+                if g == 0:
+                    dh[e, b] = bank([P, C], dh_bank(e, b), "dh%d%d" % (e, b))
+                multiply(dh[e, b][:], w_mx[e, g], slice(b * P, (b + 1) * P), g_mx[e, g], g == 0, g == last_pass)
+
+        x_plane, x_slots = {}, {}
+        for kb in range(K_BLOCKS):
+            x_plane[kb] = held([P, T], BF16, "x_plane%d" % kb)
+            nc.vector.tensor_copy(out=x_plane[kb][:], in_=x_raw[kb][:])
+        for kb in range(K_BLOCKS):
+            for e in experts:
+                x_slots[e, kb] = held([P, C], BF16, "x_slots%d%d" % (e, kb))
+                nc.scalar.activation(x_slots[e, kb][:], x_plane[kb][:].indirect(slots(e, 0, C)), COPY)
+
+        w_grouped, w_mx = {}, {}
+        for g in range(PASSES):
+            for e in experts:
+                w_grouped[e, g] = held([P, H, PACK], BF16, "w_grouped%d%d" % (e, g))
+                interleave(w_grouped[e, g][:], w_raw[e, g][:])
+        for g in range(PASSES):
+            for e in experts:
+                w_mx[e, g] = mx_tiles(H, "w%d%d" % (e, g))
+                codes, scales = w_mx[e, g]
+                quantize(codes[:], scales[:], w_grouped[e, g][:].rearrange("p i t -> p (i t)"))
+
+        for e in experts:
+            gather_g(e, 0, 1)
+        for e in experts:
+            quantize_g(e, 0)
+
+        x_grouped, x_mx = {}, {}
+        for e in experts:
+            x_grouped[e] = turn([x_slots[e, kb] for kb in range(K_BLOCKS)], dh_bank(E - 1, e), "x%d" % e)
+        for e in experts:
+            x_mx[e] = mx_tiles(K, "x%d" % e)
+            quantize(x_mx[e][0][:], x_mx[e][1][:], x_grouped[e][:])
+
+        for e in experts:
+            first_product(e, 0)
+
+        for e in experts:
+            gather_g(e, last_pass, 2 if e == E - 1 else 1)
+        for e in experts:
+            quantize_g(e, last_pass)
+            first_product(e, last_pass)
+
+        da = {}
+        for e, first in pairs:
+            for b in range(PAIR):
+                da[e, first + b] = held([P, C], BF16, "da%d%d" % (e, first + b))
+                nc.vector.scalar_tensor_tensor(
+                    out=da[e, first + b][:],
+                    in0=a_sb[e, first][:, b, :],
+                    scalar=0.0,
+                    in1=dh[e, first + b][:],
+                    op0=ALU.is_gt,
+                    op1=ALU.mult,
                 )
-            result = held([P, K // P, 2 * P], F32, "result%d%d" % (e, pair))
-            nc.scalar.copy(out=result[:], in_=acc[:])
-            nc.sync.dma_start(
-                out[e, :, pair * 2 * P : (pair + 1) * 2 * P].rearrange("(kb m) i -> m kb i", m=P), result[:]
-            )
 
-        cast_w(0, 0)
-        cast_w(1, 0)
-        cast_w(0, 1)
-        cast_w(1, 1)
-        quantize_w(0, 0)
-        quantize_w(1, 0)
-        quantize_w(0, 1)
-        quantize_w(1, 1)
-        gather_g(0, 0, 0, C)
-        gather_g(1, 0, 0, C)
-        quantize_g(0, 0, 0, C)
-        quantize_g(1, 0, 0, C)
-        gather_g(0, 1, 0, HALF)
-        gather_g(0, 1, HALF, HALF)
-        gather_g(1, 1, 0, HALF)
-        gather_g(1, 1, HALF, HALF)
-        quantize_g(0, 1, 0, HALF)
-        quantize_g(0, 1, HALF, HALF)
-        cast_x(0)
-        cast_x(1)
-        make_x(0)
-        make_x(1)
-        first_product(0, 0, 0)
-        first_product(0, 0, 1)
-        quantize_g(1, 1, 0, HALF)
-        first_product(0, 1, 0)
-        first_product(0, 1, 1)
-        quantize_g(1, 1, HALF, HALF)
-        first_product(1, 0, 0)
-        first_product(1, 0, 1)
-        quantize_x(0)
-        quantize_x(1)
-        turn_da(0, 0)
-        turn_da(0, 1)
-        first_product(1, 1, 0)
-        first_product(1, 1, 1)
-        quantize_da(0, 0)
-        quantize_da(0, 1)
-        turn_da(1, 0)
-        turn_da(1, 1)
-        second_product(0, 0)
-        second_product(0, 1)
-        quantize_da(1, 0)
-        quantize_da(1, 1)
-        second_product(1, 0)
-        second_product(1, 1)
+        da_grouped, da_mx = {}, {}
+        for e, first in pairs:
+            blocks = [da[e, first + b] for b in range(PAIR)]
+            da_grouped[e, first] = turn(blocks, dh_bank(e, first), "da%d%d" % (e, first))
+        for e, first in pairs:
+            da_mx[e, first] = mx_tiles(PAIR * P, "da%d%d" % (e, first))
+            quantize(da_mx[e, first][0][:], da_mx[e, first][1][:], da_grouped[e, first][:])
+        for e, first in pairs:
+            acc = bank([P, K_BLOCKS, PAIR * P], dh_bank(e, first + 1), "acc%d%d" % (e, first))
+            for kb in range(K_BLOCKS):
+                multiply(acc[:, kb, :], x_mx[e], slice(kb * P, (kb + 1) * P), da_mx[e, first], True, True)
+            result = held([P, K_BLOCKS, PAIR * P], F32, "result%d%d" % (e, first))
+            if (e, first) == pairs[-2]:
+                nc.vector.tensor_copy(out=result[:], in_=acc[:])
+            else:
+                nc.scalar.copy(out=result[:], in_=acc[:])
+            cols = slice(first * P, (first + PAIR) * P)
+            nc.sync.dma_start(out[e, :, cols].rearrange("(kb m) i -> m kb i", m=P), result[:])

from contextlib import ExitStack

import concourse.mybir as mybir
from concourse.masks import make_identity

K, T, E, C, H, N = 256, 1024, 2, 512, 512, 1024
FLOPS = 2 * E * C * H * (N + K)
BYTES = 4 * (K * T + N * T + H * E * C + E * N * H + E * C + E * K * H) + 2 * 128 * (E * C // 16)

F32 = mybir.dt.float32
BF16 = mybir.dt.bfloat16
U32 = mybir.dt.uint32
U16 = mybir.dt.uint16
U8 = mybir.dt.uint8
FP8X4 = mybir.dt.float8_e4m3fn_x4
ALU = mybir.AluOpType
COPY = mybir.ActivationFunctionType.Copy

P = 128
PACK = 4
PASS = P * PACK
PASSES = N // PASS
LIST_ROWS = 16
I_BLOCKS = H // P
K_BLOCKS = K // P
PAIR = 2
RUN = 2


def tile_moe_mlp_relu_kernel(tc, xT, dyT, a, w2, gate, offs, out):
    nc = tc.nc
    experts = range(E)
    pairs = [(e, first) for e in experts for first in range(0, I_BLOCKS, PAIR)]
    last_pass = PASSES - 1

    with ExitStack() as ctx:
        sbuf = ctx.enter_context(tc.tile_pool(name="sbuf", bufs=1))
        psum = ctx.enter_context(tc.psum_pool(name="psum", bufs=1))

        def held(shape, dtype, name):
            return sbuf.tile(shape, dtype, name=name, align_bytes=64)

        def bank(shape, number, name):
            return psum.tile(shape, F32, name=name, tag="bank%d" % number)

        def dh_bank(e, b):
            return I_BLOCKS * e + b

        offsets = sbuf.tile([P, E * C // LIST_ROWS], U16, name="offsets")

        def slots(e, first, count):
            start = e * C + first
            return offsets[:, start // LIST_ROWS : (start + count) // LIST_ROWS]

        gates, dy, x_raw, w_raw, a_sb = {}, {}, {}, {}, {}

        def load_gate(e):
            gates[e] = held([P, C], F32, "gate%d" % e)
            nc.sync.dma_start(gates[e][:], gate[0:P, e * C : (e + 1) * C])

        def load_dy(g, t):
            dy[g, t] = held([P, T], F32, "dy%d%d" % (g, t))
            rows = dyT[g * PASS : (g + 1) * PASS, :].rearrange("(p t) c -> p t c", t=PACK)
            nc.sync.dma_start(dy[g, t][:], rows[:, t, :])

        def load_x(kb):
            x_raw[kb] = held([P, T], F32, "x_raw%d" % kb)
            nc.sync.dma_start(x_raw[kb][:], xT[kb * P : (kb + 1) * P, :])

        def load_w(e, g):
            w_raw[e, g] = held([P, PACK, H], F32, "w_raw%d%d" % (e, g))
            rows = w2[e, g * PASS : (g + 1) * PASS, :]
            nc.sync.dma_start(w_raw[e, g][:], rows.rearrange("(p t) i -> p t i", t=PACK))

        def load_a(e, first):
            a_sb[e, first] = held([P, PAIR, C], F32, "a%d%d" % (e, first))
            rows = a[first * P : (first + PAIR) * P, e * C : (e + 1) * C]
            nc.sync.dma_start(a_sb[e, first][:], rows.rearrange("(b m) s -> m b s", m=P))

        load_dy(0, 0)
        load_gate(0)
        nc.sync.dma_start(offsets[:], offs)
        load_x(0)
        load_gate(1)
        load_x(1)
        load_dy(0, 1)
        load_dy(0, 2)
        load_dy(1, 0)
        for e in experts:
            load_w(e, 0)
        load_dy(0, 3)
        load_dy(1, 1)
        load_dy(1, 2)
        for e in experts:
            load_w(e, 1)
        load_dy(1, 3)
        for e, first in pairs:
            load_a(e, first)

        identity = held([P, P], F32, "identity")
        make_identity(nc, identity[:])

        def interleave(grouped, planes):
            nc.scalar.copy(
                out=grouped.rearrange("p (c r) t -> p c t r", r=RUN),
                in_=planes.rearrange("p t (c r) -> p c t r", r=RUN),
            )

        def mx_tiles(width, name):
            return held([P, width], U32, name + "_codes"), held([P, width], U8, name + "_scales")

        def quantize(codes, scales, grouped):
            nc.vector.quantize_mx(out=codes.bitcast(FP8X4), scales=scales, in_=grouped)

        def multiply(acc, stationary, cols, moving, start, stop):
            nc.tensor.matmul_mx(
                out=acc,
                lhsT=stationary[0][:, cols].bitcast(FP8X4),
                lhsT_scale=stationary[1][:, cols],
                rhs=moving[0][:].bitcast(FP8X4),
                rhs_scale=moving[1][:],
                start=start,
                stop=stop,
            )

        def turn(row_blocks, bank_number, name):
            turned = bank([P, 2, 2, P], bank_number, name + "_turned")
            for b, rows in enumerate(row_blocks):
                words = rows[:].bitcast(F32)
                for u in range(2):
                    nc.tensor.transpose(turned[:, b, u, :], words[:, u::2], identity[:])
            grouped = held([P, 2 * P * PACK], BF16, name + "_grouped")
            nc.scalar.copy(
                out=grouped[:].bitcast(F32).rearrange("p (b m u) -> p b m u", b=2, u=2),
                in_=turned[:].rearrange("p b u m -> p b m u"),
            )
            return grouped

        g_grouped, g_mx, dh = {}, {}, {}

        def gather_g(e, g, parts):
            width = C // parts
            gathered = held([P, PACK, C], F32, "gathered%d%d" % (e, g))
            for t in range(PACK):
                count = width if t == PACK - 1 else C
                for first in range(0, C, count):
                    nc.vector.tensor_tensor(
                        gathered[:, t, first : first + count],
                        dy[g, t][:].indirect(slots(e, first, count)),
                        gates[e][:, first : first + count],
                        ALU.mult,
                    )
            g_grouped[e, g] = []
            for first in range(0, C, width):
                grouped = held([P, width, PACK], BF16, "g_grouped%d%d_%d" % (e, g, first))
                interleave(grouped[:], gathered[:, :, first : first + width])
                g_grouped[e, g].append((slice(first, first + width), grouped))

        def quantize_g(e, g):
            g_mx[e, g] = mx_tiles(C, "g%d%d" % (e, g))
            codes, scales = g_mx[e, g]
            for cols, grouped in g_grouped[e, g]:
                quantize(codes[:, cols], scales[:, cols], grouped[:].rearrange("p s t -> p (s t)"))

        def first_product(e, g):
            for b in range(I_BLOCKS):
                if g == 0:
                    dh[e, b] = bank([P, C], dh_bank(e, b), "dh%d%d" % (e, b))
                multiply(dh[e, b][:], w_mx[e, g], slice(b * P, (b + 1) * P), g_mx[e, g], g == 0, g == last_pass)

        x_plane, x_slots = {}, {}
        for kb in range(K_BLOCKS):
            x_plane[kb] = held([P, T], BF16, "x_plane%d" % kb)
            nc.vector.tensor_copy(out=x_plane[kb][:], in_=x_raw[kb][:])
        for kb in range(K_BLOCKS):
            for e in experts:
                x_slots[e, kb] = held([P, C], BF16, "x_slots%d%d" % (e, kb))
                nc.scalar.activation(x_slots[e, kb][:], x_plane[kb][:].indirect(slots(e, 0, C)), COPY)

        w_grouped, w_mx = {}, {}
        for g in range(PASSES):
            for e in experts:
                w_grouped[e, g] = held([P, H, PACK], BF16, "w_grouped%d%d" % (e, g))
                interleave(w_grouped[e, g][:], w_raw[e, g][:])
        for g in range(PASSES):
            for e in experts:
                w_mx[e, g] = mx_tiles(H, "w%d%d" % (e, g))
                codes, scales = w_mx[e, g]
                quantize(codes[:], scales[:], w_grouped[e, g][:].rearrange("p i t -> p (i t)"))

        for e in experts:
            gather_g(e, 0, 1)
        for e in experts:
            quantize_g(e, 0)

        x_grouped, x_mx = {}, {}
        for e in experts:
            x_grouped[e] = turn([x_slots[e, kb] for kb in range(K_BLOCKS)], dh_bank(E - 1, e), "x%d" % e)
        for e in experts:
            x_mx[e] = mx_tiles(K, "x%d" % e)
            quantize(x_mx[e][0][:], x_mx[e][1][:], x_grouped[e][:])

        for e in experts:
            first_product(e, 0)

        for e in experts:
            gather_g(e, last_pass, 2 if e == E - 1 else 1)
        for e in experts:
            quantize_g(e, last_pass)
            first_product(e, last_pass)

        da = {}
        for e, first in pairs:
            for b in range(PAIR):
                da[e, first + b] = held([P, C], BF16, "da%d%d" % (e, first + b))
                nc.vector.scalar_tensor_tensor(
                    out=da[e, first + b][:],
                    in0=a_sb[e, first][:, b, :],
                    scalar=0.0,
                    in1=dh[e, first + b][:],
                    op0=ALU.is_gt,
                    op1=ALU.mult,
                )

        da_grouped, da_mx = {}, {}
        for e, first in pairs:
            blocks = [da[e, first + b] for b in range(PAIR)]
            da_grouped[e, first] = turn(blocks, dh_bank(e, first), "da%d%d" % (e, first))
        for e, first in pairs:
            da_mx[e, first] = mx_tiles(PAIR * P, "da%d%d" % (e, first))
            quantize(da_mx[e, first][0][:], da_mx[e, first][1][:], da_grouped[e, first][:])
        for e, first in pairs:
            acc = bank([P, K_BLOCKS, PAIR * P], dh_bank(e, first + 1), "acc%d%d" % (e, first))
            for kb in range(K_BLOCKS):
                multiply(acc[:, kb, :], x_mx[e], slice(kb * P, (kb + 1) * P), da_mx[e, first], True, True)
            result = held([P, K_BLOCKS, PAIR * P], F32, "result%d%d" % (e, first))
            if (e, first) == pairs[-2]:
                nc.vector.tensor_copy(out=result[:], in_=acc[:])
            else:
                nc.scalar.copy(out=result[:], in_=acc[:])
            cols = slice(first * P, (first + PAIR) * P)
            nc.sync.dma_start(out[e, :, cols].rearrange("(kb m) i -> m kb i", m=P), result[:])
